import numpy as np
import ml_dtypes


def mxq(x, axis, fmt="e4m3"):
    dtype, down = {"e4m3": (ml_dtypes.float8_e4m3fn, 7), "e5m2": (ml_dtypes.float8_e5m2, 14)}[fmt]
    v = np.moveaxis(np.asarray(x, np.float32).astype(ml_dtypes.bfloat16).astype(np.float64), axis, -1)
    blocks = v.reshape(v.shape[:-1] + (-1, 32))
    amax = np.abs(blocks).max(-1, keepdims=True)
    byte = np.maximum(np.where(amax > 0, np.frexp(amax)[1] - 1 + 127, 0) - down, 1)
    scale = np.exp2(byte - 127.0)
    codes = (blocks / scale).astype(np.float32).astype(dtype).astype(np.float64)
    return np.moveaxis((codes * scale).reshape(v.shape), -1, axis)


WIDE = False


def mx_kscale(k):
    if not WIDE:
        return np.ones(k)
    levels = np.array([10, -10, 5, -5, 0])
    if k % 512:
        return np.exp2(np.random.permutation(np.resize(levels, k // 32))).repeat(32)
    a = np.empty((k // 512, 16))
    for p in range(k // 512):
        a[p, :8] = np.random.permutation(np.resize(levels, 8))
        for g in range(8):
            far = levels[np.abs(levels - a[p, g]) >= 10]
            a[p, g + 8] = far[np.random.randint(len(far))]
    return np.exp2(a.ravel()).repeat(32)


def f64(x):
    return np.asarray(x).astype(np.float64)


def striped(idx):
    return np.tile(idx.reshape(-1, 16).T, (8, 1)).astype(np.uint16)


def unstriped(offs):
    return offs[:16].T.reshape(-1).astype(np.int64)


E2M1 = np.array([0.0, 0.5, 1.0, 1.5, 2.0, 3.0, 4.0, 6.0, -0.0, -0.5, -1.0, -1.5, -2.0, -3.0, -4.0, -6.0])


def pack_weight(w, fmt):
    k, n = w.shape
    w = f64(np.asarray(w, np.float32).astype(ml_dtypes.bfloat16)).reshape(k // 32, 32, n)
    amax = np.abs(w).max(1)
    if fmt == "e4m3":
        byte = np.frexp(amax)[1] - 1 + 127 - 7
    else:
        mant, ex = np.frexp(amax / 6.0)
        byte = np.where(mant > 0.5, ex, ex - 1) + 127
    byte = np.clip(np.where(amax > 0, byte, 1), 1, 254)
    scaled = (w * np.exp2(127.0 - byte)[:, None, :]).reshape(k, n).astype(np.float32)
    by_word = np.ascontiguousarray(scaled.reshape(k // 512, 128, 4, n).transpose(0, 1, 3, 2))
    if fmt == "e4m3":
        words = by_word.astype(ml_dtypes.float8_e4m3fn).view(np.uint8)
    else:
        c = by_word.astype(ml_dtypes.float4_e2m1fn).view(np.uint8) & 0xF
        words = (c[..., 0::2] | (c[..., 1::2] << 4)).reshape(k // 512, 128, 2 * n)
    return np.ascontiguousarray(words), np.ascontiguousarray(byte.astype(np.uint8).reshape(k // 512, 16, n))


def unpack_weight(words, scales, fmt):
    g, _, n = scales.shape
    words = np.ascontiguousarray(words).reshape(g, 128, n, -1)
    if fmt == "e4m3":
        vals = words.view(ml_dtypes.float8_e4m3fn).astype(np.float64)
    else:
        nib = np.empty((g, 128, n, 4), np.uint8)
        nib[..., 0::2] = words & 0xF
        nib[..., 1::2] = words >> 4
        vals = E2M1[nib]
    vals = vals * np.repeat(np.exp2(scales.astype(np.float64) - 127.0), 8, axis=1)[..., None]
    return vals.transpose(0, 1, 3, 2).reshape(g * 512, n)


def gelu(v):
    return 0.5 * v * (1.0 + np.tanh(np.sqrt(2.0 / np.pi) * (v + 0.044715 * v**3)))


K, H, T, S, T3, S2, T2 = 1024, 1024, 2048, 512, 2048, 512, 1024


def setup_inputs():
    n = np.random.standard_normal
    s = mx_kscale(K)[:, None]
    u = mx_kscale(H)[:, None]
    tab_words, tab_scales = pack_weight(n((K, T)) * s, "e4m3")
    tab2_words, tab2_scales = pack_weight(n((H, T3)) / np.sqrt(H) / u, "e4m3")
    w3_words, w3_scales = pack_weight(1.4 * n((K, S2)) / np.sqrt(K) / s, "e2m1")
    return {
        "tab_words": tab_words, "tab_scales": tab_scales,
        "offs": striped(np.random.permutation(T)[:S]),
        "tab2_words": tab2_words, "tab2_scales": tab2_scales,
        "offs2": striped(np.random.permutation(T3)[:S2]),
        "offs3": striped(np.random.permutation(T2)[:S]),
        "w1": (n((K, H)) / np.sqrt(K) / s * u.T).astype(np.float32),
        "b1": (0.5 * n(H) * u[:, 0]).astype(np.float32),
        "w2": (n((K, H)) / np.sqrt(K) / s * u.T).astype(np.float32),
        "b2": (0.5 * n(H) * u[:, 0]).astype(np.float32),
        "w3_words": w3_words, "w3_scales": w3_scales,
        "c3": (0.5 * n(S2)).astype(np.float32),
        "wgo": np.exp(0.3 * n((128, S))).astype(np.float32),
        "page1": n((S2, T2)).astype(np.float32),
    }


def reference(tab_words, tab_scales, offs, tab2_words, tab2_scales, offs2, offs3,
              w1, b1, w2, b2, w3_words, w3_scales, c3, wgo, page1):
    v = unpack_weight(tab_words, tab_scales, "e4m3")[:, unstriped(offs)]
    v2 = unpack_weight(tab2_words, tab2_scales, "e4m3")[:, unstriped(offs2)]
    w3 = unpack_weight(w3_words, w3_scales, "e2m1")
    h1 = (mxq(f64(w1), 0, "e4m3").T @ v) + f64(b1)[:, None]
    h2 = (mxq(f64(w2), 0, "e4m3").T @ v) + f64(b2)[:, None]
    h = mxq(np.maximum(h1, h2), 0, "e4m3")
    e = v2.T @ h
    f = np.tanh(w3.T @ v)
    y = e * f + f64(c3)[:, None]
    out = f64(page1).copy()
    out[:, unstriped(offs3)] = np.tile(f64(wgo), (S2 // 128, 1)) * y
    return out

@@ -1,0 +1,304 @@
+from contextlib import ExitStack
+
+import concourse.mybir as mybir
+
+K, H, T, S, T3, S2, T2 = 1024, 1024, 2048, 512, 2048, 512, 1024
+FLOPS = 2 * K * H * S * 2 + 2 * H * S2 * S + 2 * K * S2 * S
+
+F32 = mybir.dt.float32
+BF16 = mybir.dt.bfloat16
+I32 = mybir.dt.int32
+U32 = mybir.dt.uint32
+U16 = mybir.dt.uint16
+U8 = mybir.dt.uint8
+FP8X4 = mybir.dt.float8_e4m3fn_x4
+FP4X4 = mybir.dt.float4_e2m1fn_x4
+ACT = mybir.ActivationFunctionType
+ALU = mybir.AluOpType
+
+P = 128
+PACK = 4
+PASS = P * PACK
+PASSES = 2
+
+SCALAR_M = [128, 128, 96, 96, 64, 64, 64, 40]
+SCALAR_J = [0, 160]
+
+
+def tile_list_trick_archetype_heatpage_kernel(
+    tc, tab_words, tab_scales, offs, tab2_words, tab2_scales, offs2, offs3,
+    w1, b1, w2, b2, w3_words, w3_scales, c3, wgo, page1, out,
+):
+    nc = tc.nc
+    with ExitStack() as ctx:
+        keep = ctx.enter_context(tc.tile_pool(name="keep", bufs=1))
+        ring = ctx.enter_context(tc.tile_pool(name="ring", bufs=3))
+        stream = ctx.enter_context(tc.tile_pool(name="stream", bufs=5))
+        psum = ctx.enter_context(tc.psum_pool(name="psum", bufs=1))
+
+        def bank(n):
+            return psum.tile([P, S], F32, name="bank%d" % n)
+
+        list1 = keep.tile([P, S // 16], U16, name="list1")
+        list2 = keep.tile([P, S2 // 16], U16, name="list2")
+        list3 = keep.tile([P, S // 16], U16, name="list3")
+
+        def streamed(shape, dtype, name):
+            return stream.tile(shape, dtype, name=name, tag="streamed", align_bytes=64)
+
+        def scale_rows(shape, name):
+            rows = keep.tile(shape, U8, name=name, tag="scale_rows", align_bytes=64)
+            nc.vector.memset(rows[:].bitcast(I32), 0)
+            return rows
+
+        v_w = [keep.tile([P, S], U32, name="v_w%d" % a, align_bytes=64) for a in range(PASSES)]
+        v2_w = [keep.tile([P, S2], U32, name="v2_w%d" % a, align_bytes=64) for a in range(PASSES)]
+        v_s = keep.tile([P, S], U8, name="v_s", align_bytes=64)
+        v_s1 = keep.tile([P, S], U8, name="v_s1", align_bytes=64)
+        v2_s = keep.tile([P, S2], U8, name="v2_s", align_bytes=64)
+        b1_t = keep.tile([P, PASSES, PACK], F32, name="b1_t")
+        b2_t = keep.tile([P, PASSES, PACK], F32, name="b2_t")
+        c3_t = keep.tile([P, S2 // P], F32, name="c3_t")
+        tab_s = scale_rows([P, T], "tab_s")
+        nc.vector.memset(v_s1[:].bitcast(I32), 0)
+
+        chunks = [(wi, b, a) for b in range(PASSES) for wi in range(2) for a in range(PASSES)]
+        weights = (w1, w2)
+        raw = {}
+
+        def load_chunk(c, pieces=1):
+            wi, b, a = chunks[c]
+            width = PASS // pieces
+            raw[c] = []
+            for n in range(pieces):
+                piece = streamed([P, PACK, width], F32, "raw%d_%d" % (c, n))
+                src = weights[wi][PASS * a : PASS * (a + 1), PASS * b + width * n : PASS * b + width * (n + 1)]
+                nc.sync.dma_start(out=piece[:], in_=src.rearrange("(p j) c -> p j c", j=PACK))
+                raw[c].append(piece)
+
+        def load_words(words, a, name):
+            dst = streamed([P, T], U32, name)
+            nc.sync.dma_start(out=dst[:].bitcast(I32), in_=words[a].rearrange("p t i -> p (t i)").bitcast(I32))
+            return dst
+
+        def load_packed_scales(dst, scales, queue):
+            for q in range(4):
+                queue.dma_start(
+                    out=dst[32 * q : 32 * q + 8, :].bitcast(I32),
+                    in_=scales[:, 4 * q : 4 * q + 4, :].bitcast(I32),
+                )
+
+        def gather(dst, window, offsets):
+            nc.vector.tensor_copy(dst[:], window[:].indirect(offsets[:]))
+
+        nc.sync.dma_start(list1[:], offs)
+        nc.sync.dma_start(list2[:], offs2)
+        nc.sync.dma_start(list3[:], offs3)
+        load_chunk(0)
+        load_packed_scales(tab_s, tab_scales, nc.sync)
+        tab_w = [load_words(tab_words, 0, "tab_w0")]
+        load_chunk(1)
+        tab_w.append(load_words(tab_words, 1, "tab_w1"))
+        load_chunk(2)
+        nc.gpsimd.dma_start(out=b1_t[:], in_=b1.rearrange("(b p t) -> p b t", b=PASSES, t=PACK))
+        nc.gpsimd.dma_start(out=b2_t[:], in_=b2.rearrange("(b p t) -> p b t", b=PASSES, t=PACK))
+        with nc.allow_non_contiguous_dma(reason="one value of c3 a partition and row tile"):
+            nc.gpsimd.dma_start(out=c3_t[:], in_=c3.rearrange("(i p) -> p i", p=P))
+
+        codes, scales, grouped = {}, {}, {}
+
+        def cast_chunk(c):
+            grouped[c] = ring.tile([P, PACK, P, PACK], BF16, name="grouped", align_bytes=64)
+            pieces = len(raw[c])
+            per = P // pieces
+            share = SCALAR_M[c] // pieces
+            for n, piece in enumerate(raw[c]):
+                for engine_copy, lo, hi in ((nc.scalar.copy, 0, share), (nc.vector.tensor_copy, share, per)):
+                    if hi > lo:
+                        engine_copy(
+                            out=grouped[c][:, :, per * n + lo : per * n + hi, :].rearrange("p t m j -> p m j t"),
+                            in_=piece[:, :, PACK * lo : PACK * hi].rearrange("p j (m t) -> p m j t", t=PACK),
+                        )
+
+        def quantize_chunk(c, pieces=1):
+            codes[c] = keep.tile([P, PASS], U32, name="codes%d" % c, align_bytes=64)
+            scales[c] = keep.tile([P, PASS], U8, name="scales%d" % c, align_bytes=64)
+            flat = grouped[c][:].rearrange("p t m j -> p (t m j)")
+            width = PASS // pieces
+            for n in range(pieces):
+                cols = slice(width * n, width * (n + 1))
+                nc.vector.quantize_mx(
+                    out=codes[c][:, cols].bitcast(FP8X4),
+                    scales=scales[c][:, cols],
+                    in_=flat[:, PACK * width * n : PACK * width * (n + 1)],
+                )
+
+        banks = {}
+
+        def multiply_chunk(c):
+            wi, b, a = chunks[c]
+            for t in range(PACK):
+                if a == 0:
+                    banks[wi, b, t] = bank(PACK * wi + t)
+                cols = slice(P * t, P * (t + 1))
+                nc.tensor.matmul_mx(
+                    out=banks[wi, b, t][:],
+                    lhsT=codes[c][:, cols].bitcast(FP8X4), lhsT_scale=scales[c][:, cols],
+                    rhs=v_w[a][:].bitcast(FP8X4), rhs_scale=v_s[4 * a :, :],
+                    start=(a == 0), stop=(a == PASSES - 1),
+                )
+
+        h1 = {}
+
+        def evict_h1(b):
+            h1[b] = keep.tile([P, PACK, S], F32, name="h1_%d" % b)
+            for t in range(PACK):
+                nc.scalar.activation(
+                    out=h1[b][:, t, :], in_=banks[0, b, t][:], func=ACT.Identity, bias=b1_t[:, b, t : t + 1]
+                )
+
+        h_rows, h_codes, h_scales, h_grouped = {}, {}, {}, {}
+
+        def larger_of_two(b):
+            h_rows[b] = keep.tile([P, PACK, S], BF16, name="h_rows%d" % b)
+            for t in range(PACK):
+                nc.vector.scalar_tensor_tensor(
+                    out=h_rows[b][:, t, :], in0=banks[1, b, t][:], scalar=b2_t[:, b, t : t + 1],
+                    in1=h1[b][:, t, :], op0=ALU.add, op1=ALU.max,
+                )
+
+        def interleave_h(b):
+            h_grouped[b] = keep.tile([P, S, PACK], BF16, name="h_grouped%d" % b, align_bytes=64)
+            share = SCALAR_J[b]
+            for engine_copy, lo, hi in ((nc.scalar.copy, 0, share), (nc.vector.tensor_copy, share, S)):
+                if hi > lo:
+                    engine_copy(
+                        out=h_grouped[b][:, lo:hi, :].rearrange("p (c i) t -> p c t i", i=4),
+                        in_=h_rows[b][:, :, lo:hi].rearrange("p t (c i) -> p c t i", i=4),
+                    )
+
+        def quantize_h(b):
+            h_codes[b] = keep.tile([P, S], U32, name="h_codes%d" % b, align_bytes=64)
+            h_scales[b] = keep.tile([P, S], U8, name="h_scales%d" % b, align_bytes=64)
+            nc.vector.quantize_mx(
+                out=h_codes[b][:].bitcast(FP8X4), scales=h_scales[b][:],
+                in_=h_grouped[b][:].rearrange("p j t -> p (j t)"),
+            )
+
+        cast_chunk(0)
+        load_chunk(3)
+        quantize_chunk(0)
+        gather(v_s, tab_s, list1)
+        gather(v_w[0], tab_w[0], list1)
+        load_chunk(4)
+        nc.gpsimd.dma_start(out=v_s1[0:100, :].bitcast(I32), in_=v_s[4:104, :].bitcast(I32))
+        tab2_s = scale_rows([P, T3], "tab2_s")
+        load_packed_scales(tab2_s, tab2_scales, nc.sync)
+        multiply_chunk(0)
+        cast_chunk(1)
+        load_chunk(5)
+        quantize_chunk(1)
+        gather(v_w[1], tab_w[1], list1)
+        load_chunk(6)
+        multiply_chunk(1)
+        cast_chunk(2)
+        evict_h1(0)
+        quantize_chunk(2)
+        multiply_chunk(2)
+        gather(v2_s, tab2_s, list2)
+        w3_s = scale_rows([P, PASSES * S2], "w3_s")
+        for q in range(4):
+            nc.sync.dma_start(
+                out=w3_s[32 * q : 32 * q + 4, :].rearrange("q (a c) -> q a c", a=PASSES).bitcast(I32),
+                in_=w3_scales[:, 4 * q : 4 * q + 4, :].rearrange("a q c -> q a c").bitcast(I32),
+            )
+        cast_chunk(3)
+        load_chunk(7, pieces=2)
+        quantize_chunk(3)
+        multiply_chunk(3)
+        cast_chunk(4)
+        w3_w = streamed([P, PASSES, 2 * S2], U8, "w3_w")
+        nc.sync.dma_start(out=w3_w[:].bitcast(I32), in_=w3_words.rearrange("a p c -> p a c").bitcast(I32))
+        larger_of_two(0)
+        quantize_chunk(4)
+        multiply_chunk(4)
+        interleave_h(0)
+        cast_chunk(5)
+        tab2_w = [load_words(tab2_words, 0, "tab2_w0")]
+        quantize_h(0)
+        quantize_chunk(5)
+        multiply_chunk(5)
+        cast_chunk(6)
+        tab2_w.append(load_words(tab2_words, 1, "tab2_w1"))
+        evict_h1(1)
+        quantize_chunk(6)
+        multiply_chunk(6)
+        cast_chunk(7)
+        wgo_t = streamed([P, S], F32, "wgo_t")
+        nc.sync.dma_start(out=wgo_t[:], in_=wgo)
+        pages = []
+
+        def load_page(i):
+            pages.append(streamed([P, T2], F32, "page%d" % i))
+            nc.sync.dma_start(out=pages[i][:], in_=page1[P * i : P * (i + 1), :])
+
+        load_page(0)
+        quantize_chunk(7, pieces=PACK)
+        multiply_chunk(7)
+
+        factors = []
+        for i in range(S2 // P):
+            acc = bank(i)
+            for a in range(PASSES):
+                nc.tensor.matmul_mx(
+                    out=acc[:],
+                    lhsT=w3_w[:, a, 2 * P * i : 2 * P * (i + 1)].bitcast(FP4X4),
+                    lhsT_scale=w3_s[:, S2 * a + P * i : S2 * a + P * (i + 1)],
+                    rhs=v_w[a][:].bitcast(FP8X4), rhs_scale=(v_s, v_s1)[a][:],
+                    start=(a == 0), stop=(a == PASSES - 1),
+                )
+            factor = keep.tile([P, S], F32, name="factor%d" % i)
+            factors.append((acc, factor))
+
+        load_page(1)
+        larger_of_two(1)
+        acc, factor = factors[0]
+        nc.scalar.activation(out=factor[:], in_=acc[:], func=ACT.Tanh)
+        interleave_h(1)
+        for acc, factor in factors[1:]:
+            nc.scalar.activation(out=factor[:], in_=acc[:], func=ACT.Tanh)
+        gather(v2_w[0], tab2_w[0], list2)
+        load_page(2)
+        quantize_h(1)
+        gather(v2_w[1], tab2_w[1], list2)
+        load_page(3)
+
+        scores = [bank(PACK + i) for i in range(S2 // P)]
+        for a in range(PASSES):
+            for i in range(S2 // P):
+                cols = slice(P * i, P * (i + 1))
+                nc.tensor.matmul_mx(
+                    out=scores[i][:],
+                    lhsT=v2_w[a][:, cols].bitcast(FP8X4), lhsT_scale=v2_s[4 * a :, cols],
+                    rhs=h_codes[a][:].bitcast(FP8X4), rhs_scale=h_scales[a][:],
+                    start=(a == 0), stop=(a == PASSES - 1),
+                )
+
+        ys = []
+
+        def score(i):
+            product = ring.tile([P, S], F32, name="product")
+            nc.vector.tensor_tensor(product[:], scores[i][:], factors[i][1][:], ALU.mult)
+            y = keep.tile([P, S], F32, name="y%d" % i)
+            nc.scalar.activation(out=y[:], in_=product[:], func=ACT.Identity, bias=c3_t[:, i : i + 1])
+            ys.append(y)
+
+        def put(i):
+            nc.vector.tensor_tensor(pages[i][:].indirect(list3[:]), ys[i][:], wgo_t[:], ALU.mult)
+            nc.sync.dma_start(out=out[P * i : P * (i + 1), :], in_=pages[i][:])
+
+        score(0)
+        for i in range(S2 // P):
+            if i + 1 < S2 // P:
+                score(i + 1)
+            put(i)

@@ -21,8 +21,8 @@ PACK = 4
 PASS = P * PACK
 PASSES = 2
 
-SCALAR_M = [128, 128, 96, 96, 64, 64, 64, 40]
-SCALAR_J = [0, 160]
+SCALAR_M = [128, 0, 0, 48, 128, 64, 48, 0]
+SCALAR_J = [512, 352]
 
 
 def tile_list_trick_archetype_heatpage_kernel(
@@ -33,7 +33,6 @@ def tile_list_trick_archetype_heatpage_kernel(
     with ExitStack() as ctx:
         keep = ctx.enter_context(tc.tile_pool(name="keep", bufs=1))
         ring = ctx.enter_context(tc.tile_pool(name="ring", bufs=3))
-        stream = ctx.enter_context(tc.tile_pool(name="stream", bufs=5))
         psum = ctx.enter_context(tc.psum_pool(name="psum", bufs=1))
 
         def bank(n):
@@ -42,25 +41,26 @@ def tile_list_trick_archetype_heatpage_kernel(
         list1 = keep.tile([P, S // 16], U16, name="list1")
         list2 = keep.tile([P, S2 // 16], U16, name="list2")
         list3 = keep.tile([P, S // 16], U16, name="list3")
-
-        def streamed(shape, dtype, name):
-            return stream.tile(shape, dtype, name=name, tag="streamed", align_bytes=64)
-
-        def scale_rows(shape, name):
-            rows = keep.tile(shape, U8, name=name, tag="scale_rows", align_bytes=64)
-            nc.vector.memset(rows[:].bitcast(I32), 0)
-            return rows
-
+        tab_w = [keep.tile([P, T], U32, name="tab_w%d" % a) for a in range(PASSES)]
+        tab2_w = [keep.tile([P, T3], U32, name="tab2_w%d" % a) for a in range(PASSES)]
+        tab_s = keep.tile([P, T], U8, name="tab_s")
+        tab2_s = keep.tile([P, T3], U8, name="tab2_s")
+        w3_w = keep.tile([P, PASSES, 2 * S2], U8, name="w3_w", align_bytes=64)
+        w3_s = keep.tile([P, PASSES, S2], U8, name="w3_s", align_bytes=64)
         v_w = [keep.tile([P, S], U32, name="v_w%d" % a, align_bytes=64) for a in range(PASSES)]
-        v2_w = [keep.tile([P, S2], U32, name="v2_w%d" % a, align_bytes=64) for a in range(PASSES)]
+        v2_first = keep.tile([P, S2], U32, name="v2_first", align_bytes=64)
+        v2_last = [keep.tile([P, P], U32, name="v2_last%d" % i, align_bytes=64) for i in range(S2 // P)]
         v_s = keep.tile([P, S], U8, name="v_s", align_bytes=64)
         v_s1 = keep.tile([P, S], U8, name="v_s1", align_bytes=64)
         v2_s = keep.tile([P, S2], U8, name="v2_s", align_bytes=64)
         b1_t = keep.tile([P, PASSES, PACK], F32, name="b1_t")
         b2_t = keep.tile([P, PASSES, PACK], F32, name="b2_t")
         c3_t = keep.tile([P, S2 // P], F32, name="c3_t")
-        tab_s = scale_rows([P, T], "tab_s")
-        nc.vector.memset(v_s1[:].bitcast(I32), 0)
+        wgo_t = keep.tile([P, S], F32, name="wgo_t")
+        pages = [keep.tile([P, T2], F32, name="page%d" % i) for i in range(S2 // P)]
+
+        for plane in (tab_s[:], tab2_s[:], w3_s[:].rearrange("p a c -> p (a c)"), v_s1[:]):
+            nc.vector.memset(plane.bitcast(I32), 0)
 
         chunks = [(wi, b, a) for b in range(PASSES) for wi in range(2) for a in range(PASSES)]
         weights = (w1, w2)
@@ -71,15 +71,13 @@ def tile_list_trick_archetype_heatpage_kernel(
             width = PASS // pieces
             raw[c] = []
             for n in range(pieces):
-                piece = streamed([P, PACK, width], F32, "raw%d_%d" % (c, n))
+                piece = keep.tile([P, PACK, width], F32, name="raw%d_%d" % (c, n))
                 src = weights[wi][PASS * a : PASS * (a + 1), PASS * b + width * n : PASS * b + width * (n + 1)]
                 nc.sync.dma_start(out=piece[:], in_=src.rearrange("(p j) c -> p j c", j=PACK))
                 raw[c].append(piece)
 
-        def load_words(words, a, name):
-            dst = streamed([P, T], U32, name)
+        def load_words(dst, words, a):
             nc.sync.dma_start(out=dst[:].bitcast(I32), in_=words[a].rearrange("p t i -> p (t i)").bitcast(I32))
-            return dst
 
         def load_packed_scales(dst, scales, queue):
             for q in range(4):
@@ -88,20 +86,35 @@ def tile_list_trick_archetype_heatpage_kernel(
                     in_=scales[:, 4 * q : 4 * q + 4, :].bitcast(I32),
                 )
 
-        def gather(dst, window, offsets):
-            nc.vector.tensor_copy(dst[:], window[:].indirect(offsets[:]))
-
         nc.sync.dma_start(list1[:], offs)
         nc.sync.dma_start(list2[:], offs2)
         nc.sync.dma_start(list3[:], offs3)
         load_chunk(0)
         load_packed_scales(tab_s, tab_scales, nc.sync)
-        tab_w = [load_words(tab_words, 0, "tab_w0")]
+        load_words(tab_w[0], tab_words, 0)
         load_chunk(1)
-        tab_w.append(load_words(tab_words, 1, "tab_w1"))
+        nc.sync.dma_start(out=b1_t[:], in_=b1.rearrange("(b p t) -> p b t", b=PASSES, t=PACK))
+        load_words(tab_w[1], tab_words, 1)
+        load_packed_scales(tab2_s, tab2_scales, nc.sync)
         load_chunk(2)
-        nc.gpsimd.dma_start(out=b1_t[:], in_=b1.rearrange("(b p t) -> p b t", b=PASSES, t=PACK))
-        nc.gpsimd.dma_start(out=b2_t[:], in_=b2.rearrange("(b p t) -> p b t", b=PASSES, t=PACK))
+        nc.sync.dma_start(out=b2_t[:], in_=b2.rearrange("(b p t) -> p b t", b=PASSES, t=PACK))
+        for c in range(3, 7):
+            load_chunk(c)
+        load_chunk(7, pieces=2)
+        for q in range(4):
+            nc.sync.dma_start(
+                out=w3_s[32 * q : 32 * q + 4, :, :].bitcast(I32),
+                in_=w3_scales[:, 4 * q : 4 * q + 4, :].rearrange("a q c -> q a c").bitcast(I32),
+            )
+        nc.sync.dma_start(
+            out=w3_w[:].bitcast(I32), in_=w3_words.rearrange("a p c -> p a c").bitcast(I32)
+        )
+        load_words(tab2_w[0], tab2_words, 0)
+        load_words(tab2_w[1], tab2_words, 1)
+        nc.sync.dma_start(out=wgo_t[:], in_=wgo)
+        for i in range(S2 // P):
+            nc.sync.dma_start(out=pages[i][:], in_=page1[P * i : P * (i + 1), :])
+
         with nc.allow_non_contiguous_dma(reason="one value of c3 a partition and row tile"):
             nc.gpsimd.dma_start(out=c3_t[:], in_=c3.rearrange("(i p) -> p i", p=P))
 
@@ -170,7 +183,8 @@ def tile_list_trick_archetype_heatpage_kernel(
         def interleave_h(b):
             h_grouped[b] = keep.tile([P, S, PACK], BF16, name="h_grouped%d" % b, align_bytes=64)
             share = SCALAR_J[b]
-            for engine_copy, lo, hi in ((nc.scalar.copy, 0, share), (nc.vector.tensor_copy, share, S)):
+            parts = [(nc.scalar.copy, lo, min(lo + P, share)) for lo in range(0, share, P)]
+            for engine_copy, lo, hi in parts + [(nc.vector.tensor_copy, share, S)]:
                 if hi > lo:
                     engine_copy(
                         out=h_grouped[b][:, lo:hi, :].rearrange("p (c i) t -> p c t i", i=4),
@@ -185,110 +199,94 @@ def tile_list_trick_archetype_heatpage_kernel(
                 in_=h_grouped[b][:].rearrange("p j t -> p (j t)"),
             )
 
+        def gather(dst, window, offsets):
+            nc.vector.tensor_copy(dst[:], window[:].indirect(offsets[:]))
+
         cast_chunk(0)
-        load_chunk(3)
-        quantize_chunk(0)
         gather(v_s, tab_s, list1)
+        quantize_chunk(0)
         gather(v_w[0], tab_w[0], list1)
-        load_chunk(4)
         nc.gpsimd.dma_start(out=v_s1[0:100, :].bitcast(I32), in_=v_s[4:104, :].bitcast(I32))
-        tab2_s = scale_rows([P, T3], "tab2_s")
-        load_packed_scales(tab2_s, tab2_scales, nc.sync)
         multiply_chunk(0)
         cast_chunk(1)
-        load_chunk(5)
         quantize_chunk(1)
         gather(v_w[1], tab_w[1], list1)
-        load_chunk(6)
         multiply_chunk(1)
-        cast_chunk(2)
+        gather(v2_s, tab2_s, list2)
         evict_h1(0)
+        cast_chunk(2)
         quantize_chunk(2)
         multiply_chunk(2)
-        gather(v2_s, tab2_s, list2)
-        w3_s = scale_rows([P, PASSES * S2], "w3_s")
-        for q in range(4):
-            nc.sync.dma_start(
-                out=w3_s[32 * q : 32 * q + 4, :].rearrange("q (a c) -> q a c", a=PASSES).bitcast(I32),
-                in_=w3_scales[:, 4 * q : 4 * q + 4, :].rearrange("a q c -> q a c").bitcast(I32),
-            )
         cast_chunk(3)
-        load_chunk(7, pieces=2)
         quantize_chunk(3)
         multiply_chunk(3)
         cast_chunk(4)
-        w3_w = streamed([P, PASSES, 2 * S2], U8, "w3_w")
-        nc.sync.dma_start(out=w3_w[:].bitcast(I32), in_=w3_words.rearrange("a p c -> p a c").bitcast(I32))
         larger_of_two(0)
         quantize_chunk(4)
         multiply_chunk(4)
-        interleave_h(0)
         cast_chunk(5)
-        tab2_w = [load_words(tab2_words, 0, "tab2_w0")]
-        quantize_h(0)
         quantize_chunk(5)
         multiply_chunk(5)
         cast_chunk(6)
-        tab2_w.append(load_words(tab2_words, 1, "tab2_w1"))
-        evict_h1(1)
         quantize_chunk(6)
+        evict_h1(1)
         multiply_chunk(6)
         cast_chunk(7)
-        wgo_t = streamed([P, S], F32, "wgo_t")
-        nc.sync.dma_start(out=wgo_t[:], in_=wgo)
-        pages = []
-
-        def load_page(i):
-            pages.append(streamed([P, T2], F32, "page%d" % i))
-            nc.sync.dma_start(out=pages[i][:], in_=page1[P * i : P * (i + 1), :])
-
-        load_page(0)
         quantize_chunk(7, pieces=PACK)
         multiply_chunk(7)
 
-        factors = []
-        for i in range(S2 // P):
+        factors = {}
+
+        def bounded_factor(i):
             acc = bank(i)
             for a in range(PASSES):
                 nc.tensor.matmul_mx(
                     out=acc[:],
                     lhsT=w3_w[:, a, 2 * P * i : 2 * P * (i + 1)].bitcast(FP4X4),
-                    lhsT_scale=w3_s[:, S2 * a + P * i : S2 * a + P * (i + 1)],
+                    lhsT_scale=w3_s[:, a, P * i : P * (i + 1)],
                     rhs=v_w[a][:].bitcast(FP8X4), rhs_scale=(v_s, v_s1)[a][:],
                     start=(a == 0), stop=(a == PASSES - 1),
                 )
-            factor = keep.tile([P, S], F32, name="factor%d" % i)
-            factors.append((acc, factor))
+            factors[i] = keep.tile([P, S], F32, name="factor%d" % i)
+            nc.scalar.activation(out=factors[i][:], in_=acc[:], func=ACT.Tanh)
 
-        load_page(1)
-        larger_of_two(1)
-        acc, factor = factors[0]
-        nc.scalar.activation(out=factor[:], in_=acc[:], func=ACT.Tanh)
-        interleave_h(1)
-        for acc, factor in factors[1:]:
-            nc.scalar.activation(out=factor[:], in_=acc[:], func=ACT.Tanh)
-        gather(v2_w[0], tab2_w[0], list2)
-        load_page(2)
-        quantize_h(1)
-        gather(v2_w[1], tab2_w[1], list2)
-        load_page(3)
+        def gather_archetypes(i):
+            nc.vector.tensor_copy(
+                v2_last[i][:], tab2_w[1][:].indirect(list2[:, (P // 16) * i : (P // 16) * (i + 1)])
+            )
 
-        scores = [bank(PACK + i) for i in range(S2 // P)]
-        for a in range(PASSES):
-            for i in range(S2 // P):
-                cols = slice(P * i, P * (i + 1))
+        scores = {}
+
+        def multiply_scores(i):
+            scores[i] = bank(PACK + i)
+            cols = slice(P * i, P * (i + 1))
+            for a in range(PASSES):
                 nc.tensor.matmul_mx(
                     out=scores[i][:],
-                    lhsT=v2_w[a][:, cols].bitcast(FP8X4), lhsT_scale=v2_s[4 * a :, cols],
+                    lhsT=(v2_first[:, cols], v2_last[i][:])[a].bitcast(FP8X4), lhsT_scale=v2_s[4 * a :, cols],
                     rhs=h_codes[a][:].bitcast(FP8X4), rhs_scale=h_scales[a][:],
                     start=(a == 0), stop=(a == PASSES - 1),
                 )
+
+        larger_of_two(1)
+        interleave_h(0)
+        quantize_h(0)
+        interleave_h(1)
+        gather(v2_first, tab2_w[0], list2)
+        gather_archetypes(0)
+        quantize_h(1)
+        bounded_factor(0)
+        for i in range(S2 // P):
+            multiply_scores(i)
+            if i + 1 < S2 // P:
+                gather_archetypes(i + 1)
+                bounded_factor(i + 1)
 
         ys = []
 
         def score(i):
             product = ring.tile([P, S], F32, name="product")
-            nc.vector.tensor_tensor(product[:], scores[i][:], factors[i][1][:], ALU.mult)
+            nc.vector.tensor_tensor(product[:], scores[i][:], factors[i][:], ALU.mult)
             y = keep.tile([P, S], F32, name="y%d" % i)
             nc.scalar.activation(out=y[:], in_=product[:], func=ACT.Identity, bias=c3_t[:, i : i + 1])
             ys.append(y)

from contextlib import ExitStack

import concourse.mybir as mybir

K, H, T, S, T3, S2, T2 = 1024, 1024, 2048, 512, 2048, 512, 1024
FLOPS = 2 * K * H * S * 2 + 2 * H * S2 * S + 2 * K * S2 * S

F32 = mybir.dt.float32
BF16 = mybir.dt.bfloat16
I32 = mybir.dt.int32
U32 = mybir.dt.uint32
U16 = mybir.dt.uint16
U8 = mybir.dt.uint8
FP8X4 = mybir.dt.float8_e4m3fn_x4
FP4X4 = mybir.dt.float4_e2m1fn_x4
ACT = mybir.ActivationFunctionType
ALU = mybir.AluOpType

P = 128
PACK = 4
PASS = P * PACK
PASSES = 2

SCALAR_M = [128, 0, 0, 48, 128, 64, 48, 0]
SCALAR_J = [512, 352]


def tile_list_trick_archetype_heatpage_kernel(
    tc, tab_words, tab_scales, offs, tab2_words, tab2_scales, offs2, offs3,
    w1, b1, w2, b2, w3_words, w3_scales, c3, wgo, page1, out,
):
    nc = tc.nc
    with ExitStack() as ctx:
        keep = ctx.enter_context(tc.tile_pool(name="keep", bufs=1))
        ring = ctx.enter_context(tc.tile_pool(name="ring", bufs=3))
        psum = ctx.enter_context(tc.psum_pool(name="psum", bufs=1))

        def bank(n):
            return psum.tile([P, S], F32, name="bank%d" % n)

        list1 = keep.tile([P, S // 16], U16, name="list1")
        list2 = keep.tile([P, S2 // 16], U16, name="list2")
        list3 = keep.tile([P, S // 16], U16, name="list3")
        tab_w = [keep.tile([P, T], U32, name="tab_w%d" % a) for a in range(PASSES)]
        tab2_w = [keep.tile([P, T3], U32, name="tab2_w%d" % a) for a in range(PASSES)]
        tab_s = keep.tile([P, T], U8, name="tab_s")
        tab2_s = keep.tile([P, T3], U8, name="tab2_s")
        w3_w = keep.tile([P, PASSES, 2 * S2], U8, name="w3_w", align_bytes=64)
        w3_s = keep.tile([P, PASSES, S2], U8, name="w3_s", align_bytes=64)
        v_w = [keep.tile([P, S], U32, name="v_w%d" % a, align_bytes=64) for a in range(PASSES)]
        v2_first = keep.tile([P, S2], U32, name="v2_first", align_bytes=64)
        v2_last = [keep.tile([P, P], U32, name="v2_last%d" % i, align_bytes=64) for i in range(S2 // P)]
        v_s = keep.tile([P, S], U8, name="v_s", align_bytes=64)
        v_s1 = keep.tile([P, S], U8, name="v_s1", align_bytes=64)
        v2_s = keep.tile([P, S2], U8, name="v2_s", align_bytes=64)
        b1_t = keep.tile([P, PASSES, PACK], F32, name="b1_t")
        b2_t = keep.tile([P, PASSES, PACK], F32, name="b2_t")
        c3_t = keep.tile([P, S2 // P], F32, name="c3_t")
        wgo_t = keep.tile([P, S], F32, name="wgo_t")
        pages = [keep.tile([P, T2], F32, name="page%d" % i) for i in range(S2 // P)]

        for plane in (tab_s[:], tab2_s[:], w3_s[:].rearrange("p a c -> p (a c)"), v_s1[:]):
            nc.vector.memset(plane.bitcast(I32), 0)

        chunks = [(wi, b, a) for b in range(PASSES) for wi in range(2) for a in range(PASSES)]
        weights = (w1, w2)
        raw = {}

        def load_chunk(c, pieces=1):
            wi, b, a = chunks[c]
            width = PASS // pieces
            raw[c] = []
            for n in range(pieces):
                piece = keep.tile([P, PACK, width], F32, name="raw%d_%d" % (c, n))
                src = weights[wi][PASS * a : PASS * (a + 1), PASS * b + width * n : PASS * b + width * (n + 1)]
                nc.sync.dma_start(out=piece[:], in_=src.rearrange("(p j) c -> p j c", j=PACK))
                raw[c].append(piece)

        def load_words(dst, words, a):
            nc.sync.dma_start(out=dst[:].bitcast(I32), in_=words[a].rearrange("p t i -> p (t i)").bitcast(I32))

        def load_packed_scales(dst, scales, queue):
            for q in range(4):
                queue.dma_start(
                    out=dst[32 * q : 32 * q + 8, :].bitcast(I32),
                    in_=scales[:, 4 * q : 4 * q + 4, :].bitcast(I32),
                )

        nc.sync.dma_start(list1[:], offs)
        nc.sync.dma_start(list2[:], offs2)
        nc.sync.dma_start(list3[:], offs3)
        load_chunk(0)
        load_packed_scales(tab_s, tab_scales, nc.sync)
        load_words(tab_w[0], tab_words, 0)
        load_chunk(1)
        nc.sync.dma_start(out=b1_t[:], in_=b1.rearrange("(b p t) -> p b t", b=PASSES, t=PACK))
        load_words(tab_w[1], tab_words, 1)
        load_packed_scales(tab2_s, tab2_scales, nc.sync)
        load_chunk(2)
        nc.sync.dma_start(out=b2_t[:], in_=b2.rearrange("(b p t) -> p b t", b=PASSES, t=PACK))
        for c in range(3, 7):
            load_chunk(c)
        load_chunk(7, pieces=2)
        for q in range(4):
            nc.sync.dma_start(
                out=w3_s[32 * q : 32 * q + 4, :, :].bitcast(I32),
                in_=w3_scales[:, 4 * q : 4 * q + 4, :].rearrange("a q c -> q a c").bitcast(I32),
            )
        nc.sync.dma_start(
            out=w3_w[:].bitcast(I32), in_=w3_words.rearrange("a p c -> p a c").bitcast(I32)
        )
        load_words(tab2_w[0], tab2_words, 0)
        load_words(tab2_w[1], tab2_words, 1)
        nc.sync.dma_start(out=wgo_t[:], in_=wgo)
        for i in range(S2 // P):
            nc.sync.dma_start(out=pages[i][:], in_=page1[P * i : P * (i + 1), :])

        with nc.allow_non_contiguous_dma(reason="one value of c3 a partition and row tile"):
            nc.gpsimd.dma_start(out=c3_t[:], in_=c3.rearrange("(i p) -> p i", p=P))

        codes, scales, grouped = {}, {}, {}

        def cast_chunk(c):
            grouped[c] = ring.tile([P, PACK, P, PACK], BF16, name="grouped", align_bytes=64)
            pieces = len(raw[c])
            per = P // pieces
            share = SCALAR_M[c] // pieces
            for n, piece in enumerate(raw[c]):
                for engine_copy, lo, hi in ((nc.scalar.copy, 0, share), (nc.vector.tensor_copy, share, per)):
                    if hi > lo:
                        engine_copy(
                            out=grouped[c][:, :, per * n + lo : per * n + hi, :].rearrange("p t m j -> p m j t"),
                            in_=piece[:, :, PACK * lo : PACK * hi].rearrange("p j (m t) -> p m j t", t=PACK),
                        )

        def quantize_chunk(c, pieces=1):
            codes[c] = keep.tile([P, PASS], U32, name="codes%d" % c, align_bytes=64)
            scales[c] = keep.tile([P, PASS], U8, name="scales%d" % c, align_bytes=64)
            flat = grouped[c][:].rearrange("p t m j -> p (t m j)")
            width = PASS // pieces
            for n in range(pieces):
                cols = slice(width * n, width * (n + 1))
                nc.vector.quantize_mx(
                    out=codes[c][:, cols].bitcast(FP8X4),
                    scales=scales[c][:, cols],
                    in_=flat[:, PACK * width * n : PACK * width * (n + 1)],
                )

        banks = {}

        def multiply_chunk(c):
            wi, b, a = chunks[c]
            for t in range(PACK):
                if a == 0:
                    banks[wi, b, t] = bank(PACK * wi + t)
                cols = slice(P * t, P * (t + 1))
                nc.tensor.matmul_mx(
                    out=banks[wi, b, t][:],
                    lhsT=codes[c][:, cols].bitcast(FP8X4), lhsT_scale=scales[c][:, cols],
                    rhs=v_w[a][:].bitcast(FP8X4), rhs_scale=v_s[4 * a :, :],
                    start=(a == 0), stop=(a == PASSES - 1),
                )

        h1 = {}

        def evict_h1(b):
            h1[b] = keep.tile([P, PACK, S], F32, name="h1_%d" % b)
            for t in range(PACK):
                nc.scalar.activation(
                    out=h1[b][:, t, :], in_=banks[0, b, t][:], func=ACT.Identity, bias=b1_t[:, b, t : t + 1]
                )

        h_rows, h_codes, h_scales, h_grouped = {}, {}, {}, {}

        def larger_of_two(b):
            h_rows[b] = keep.tile([P, PACK, S], BF16, name="h_rows%d" % b)
            for t in range(PACK):
                nc.vector.scalar_tensor_tensor(
                    out=h_rows[b][:, t, :], in0=banks[1, b, t][:], scalar=b2_t[:, b, t : t + 1],
                    in1=h1[b][:, t, :], op0=ALU.add, op1=ALU.max,
                )

        def interleave_h(b):
            h_grouped[b] = keep.tile([P, S, PACK], BF16, name="h_grouped%d" % b, align_bytes=64)
            share = SCALAR_J[b]
            parts = [(nc.scalar.copy, lo, min(lo + P, share)) for lo in range(0, share, P)]
            for engine_copy, lo, hi in parts + [(nc.vector.tensor_copy, share, S)]:
                if hi > lo:
                    engine_copy(
                        out=h_grouped[b][:, lo:hi, :].rearrange("p (c i) t -> p c t i", i=4),
                        in_=h_rows[b][:, :, lo:hi].rearrange("p t (c i) -> p c t i", i=4),
                    )

        def quantize_h(b):
            h_codes[b] = keep.tile([P, S], U32, name="h_codes%d" % b, align_bytes=64)
            h_scales[b] = keep.tile([P, S], U8, name="h_scales%d" % b, align_bytes=64)
            nc.vector.quantize_mx(
                out=h_codes[b][:].bitcast(FP8X4), scales=h_scales[b][:],
                in_=h_grouped[b][:].rearrange("p j t -> p (j t)"),
            )

        def gather(dst, window, offsets):
            nc.vector.tensor_copy(dst[:], window[:].indirect(offsets[:]))

        cast_chunk(0)
        gather(v_s, tab_s, list1)
        quantize_chunk(0)
        gather(v_w[0], tab_w[0], list1)
        nc.gpsimd.dma_start(out=v_s1[0:100, :].bitcast(I32), in_=v_s[4:104, :].bitcast(I32))
        multiply_chunk(0)
        cast_chunk(1)
        quantize_chunk(1)
        gather(v_w[1], tab_w[1], list1)
        multiply_chunk(1)
        gather(v2_s, tab2_s, list2)
        evict_h1(0)
        cast_chunk(2)
        quantize_chunk(2)
        multiply_chunk(2)
        cast_chunk(3)
        quantize_chunk(3)
        multiply_chunk(3)
        cast_chunk(4)
        larger_of_two(0)
        quantize_chunk(4)
        multiply_chunk(4)
        cast_chunk(5)
        quantize_chunk(5)
        multiply_chunk(5)
        cast_chunk(6)
        quantize_chunk(6)
        evict_h1(1)
        multiply_chunk(6)
        cast_chunk(7)
        quantize_chunk(7, pieces=PACK)
        multiply_chunk(7)

        factors = {}

        def bounded_factor(i):
            acc = bank(i)
            for a in range(PASSES):
                nc.tensor.matmul_mx(
                    out=acc[:],
                    lhsT=w3_w[:, a, 2 * P * i : 2 * P * (i + 1)].bitcast(FP4X4),
                    lhsT_scale=w3_s[:, a, P * i : P * (i + 1)],
                    rhs=v_w[a][:].bitcast(FP8X4), rhs_scale=(v_s, v_s1)[a][:],
                    start=(a == 0), stop=(a == PASSES - 1),
                )
            factors[i] = keep.tile([P, S], F32, name="factor%d" % i)
            nc.scalar.activation(out=factors[i][:], in_=acc[:], func=ACT.Tanh)

        def gather_archetypes(i):
            nc.vector.tensor_copy(
                v2_last[i][:], tab2_w[1][:].indirect(list2[:, (P // 16) * i : (P // 16) * (i + 1)])
            )

        scores = {}

        def multiply_scores(i):
            scores[i] = bank(PACK + i)
            cols = slice(P * i, P * (i + 1))
            for a in range(PASSES):
                nc.tensor.matmul_mx(
                    out=scores[i][:],
                    lhsT=(v2_first[:, cols], v2_last[i][:])[a].bitcast(FP8X4), lhsT_scale=v2_s[4 * a :, cols],
                    rhs=h_codes[a][:].bitcast(FP8X4), rhs_scale=h_scales[a][:],
                    start=(a == 0), stop=(a == PASSES - 1),
                )

        larger_of_two(1)
        interleave_h(0)
        quantize_h(0)
        interleave_h(1)
        gather(v2_first, tab2_w[0], list2)
        gather_archetypes(0)
        quantize_h(1)
        bounded_factor(0)
        for i in range(S2 // P):
            multiply_scores(i)
            if i + 1 < S2 // P:
                gather_archetypes(i + 1)
                bounded_factor(i + 1)

        ys = []

        def score(i):
            product = ring.tile([P, S], F32, name="product")
            nc.vector.tensor_tensor(product[:], scores[i][:], factors[i][:], ALU.mult)
            y = keep.tile([P, S], F32, name="y%d" % i)
            nc.scalar.activation(out=y[:], in_=product[:], func=ACT.Identity, bias=c3_t[:, i : i + 1])
            ys.append(y)

        def put(i):
            nc.vector.tensor_tensor(pages[i][:].indirect(list3[:]), ys[i][:], wgo_t[:], ALU.mult)
            nc.sync.dma_start(out=out[P * i : P * (i + 1), :], in_=pages[i][:])

        score(0)
        for i in range(S2 // P):
            if i + 1 < S2 // P:
                score(i + 1)
            put(i)
